import numpy as np
import ml_dtypes


def mxq(x, axis, fmt="e4m3"):
    dtype, down = {"e4m3": (ml_dtypes.float8_e4m3fn, 7), "e5m2": (ml_dtypes.float8_e5m2, 14)}[fmt]
    v = np.moveaxis(np.asarray(x, np.float32).astype(ml_dtypes.bfloat16).astype(np.float64), axis, -1)
    blocks = v.reshape(v.shape[:-1] + (-1, 32))
    amax = np.abs(blocks).max(-1, keepdims=True)
    byte = np.maximum(np.where(amax > 0, np.frexp(amax)[1] - 1 + 127, 0) - down, 1)
    scale = np.exp2(byte - 127.0)
    codes = (blocks / scale).astype(np.float32).astype(dtype).astype(np.float64)
    return np.moveaxis((codes * scale).reshape(v.shape), -1, axis)


WIDE = False


def mx_kscale(k):
    if not WIDE:
        return np.ones(k)
    levels = np.array([10, -10, 5, -5, 0])
    if k % 512:
        return np.exp2(np.random.permutation(np.resize(levels, k // 32))).repeat(32)
    a = np.empty((k // 512, 16))
    for p in range(k // 512):
        a[p, :8] = np.random.permutation(np.resize(levels, 8))
        for g in range(8):
            far = levels[np.abs(levels - a[p, g]) >= 10]
            a[p, g + 8] = far[np.random.randint(len(far))]
    return np.exp2(a.ravel()).repeat(32)


BF16 = ml_dtypes.bfloat16


def bf(x):
    return np.asarray(x, np.float32).astype(BF16)


def f64(x):
    return np.asarray(x).astype(np.float64)


B, T, C, P, M, E = 1, 1024, 512, 128, 512, 1024
N = T // C


def draw0():
    s, t = mx_kscale(T), mx_kscale(M)
    return {
        "q1": bf(np.random.standard_normal((B, T, P))),
        "k1": bf(np.random.standard_normal((B, T, P))),
        "q2": bf(np.random.standard_normal((B, T, M)) / np.sqrt(M) / t),
        "k2": bf(np.random.standard_normal((B, T, M)) / np.sqrt(T) * t / s[:, None]),
        "v": bf(np.random.standard_normal((B, T, E)) * s[:, None]),
        "gt": bf(np.random.standard_normal(T) / np.sqrt(C) / s),
        "u": bf(np.random.standard_normal((B, T, E))),
    }


def chunk_quadratic(q1, k1, vq, gt):
    q1c = f64(q1).reshape(B, N, C, P)
    k1c = f64(k1).reshape(B, N, C, P)
    vc = vq.reshape(B, N, C, E)
    gc = f64(gt).reshape(N, C)
    z = q1c @ k1c.transpose(0, 1, 3, 2) / np.sqrt(P)
    a = np.maximum(z, 0.0) ** 2 * gc[None, :, None, :]
    oq = mxq(a, 3, "e4m3") @ vc
    return oq.reshape(B, T, E)


def global_linear(q2, k2, vq):
    m = mxq(f64(k2), 1, "e4m3").transpose(0, 2, 1) @ vq
    return mxq(f64(q2), 2, "e4m3") @ mxq(m, 1, "e4m3")


def core(q1, k1, q2, k2, v, gt, u):
    vq = mxq(f64(v), 1, "e4m3")
    oq = chunk_quadratic(q1, k1, vq, gt)
    ol = global_linear(q2, k2, vq)
    return f64(u) * (oq + ol)


def e4m3fn_bytes(y):
    return np.clip(np.asarray(y, np.float64), -448.0, 448.0).astype(np.float32).astype(ml_dtypes.float8_e4m3fn).view(np.uint8)


def e4m3fn_values(b):
    return np.asarray(b, np.uint8).view(ml_dtypes.float8_e4m3fn).astype(np.float64)


def setup_inputs():
    d = draw0()
    x0 = np.asarray(d['v']).astype(np.float64)
    s = (np.max(np.abs(x0), axis=(0, 2), keepdims=True) / 448.0).astype(np.float32)
    out = {}
    for k, v in d.items():
        if k == 'v':
            out['v_bytes'] = e4m3fn_bytes(x0 / s.astype(np.float64))
            out['v_scale'] = s
        else:
            out[k] = v
    return out


def reference(q1, k1, q2, k2, v_bytes, v_scale, gt, u):
    return core(q1, k1, q2, k2, e4m3fn_values(v_bytes) * v_scale.astype(np.float64), gt, u)

@@ -1,0 +1,370 @@
+from contextlib import ExitStack
+
+import concourse.mybir as mybir
+from concourse.masks import make_identity
+
+T, C, D, M, E = 1024, 512, 128, 512, 1024
+FLOPS = 2 * T * C * D + 2 * T * C * E + 2 * T * M * E + 2 * T * M * E
+
+F32 = mybir.dt.float32
+BF16 = mybir.dt.bfloat16
+U32 = mybir.dt.uint32
+U8 = mybir.dt.uint8
+FP8 = mybir.dt.float8_e4m3fn
+FP8X4 = mybir.dt.float8_e4m3fn_x4
+ALU = mybir.AluOpType
+ACT = mybir.ActivationFunctionType
+
+P = 128
+PACK = 4
+HALF = 512
+CHUNKS = T // C
+HALVES = E // HALF
+PART = 256
+PARTS = E // PART
+
+
+def tile_flashmixedchunkrelusquaredplusgloballine_kernel(tc, q1, k1, q2, k2, v_bytes, v_scale, gt, u, out):
+    nc = tc.nc
+
+    def rows(x, c):
+        return x[0, c * C:(c + 1) * C, :].rearrange("(p t) w -> p t w", t=PACK)
+
+    with ExitStack() as ctx:
+        keep = ctx.enter_context(tc.tile_pool(name="keep", bufs=1))
+        stage = ctx.enter_context(tc.tile_pool(name="stage", bufs=2))
+        psum = ctx.enter_context(tc.psum_pool(name="psum", bufs=1))
+        ctx.enter_context(tc.manual_schedule())
+
+        free_banks = list(range(8))
+        owner = {}
+
+        def kept(name, shape, dtype):
+            return keep.tile(shape, dtype, name=name, align_bytes=64)
+
+        def bank(name, shape, dtype):
+            owner[name] = free_banks.pop(0)
+            return psum.tile(shape, dtype, name=name, tag="bank%d" % owner[name])
+
+        def release(name):
+            free_banks.append(owner[name])
+
+        ident_bf = kept("ident_bf", [P, P], BF16)
+        ident_f32 = kept("ident_f32", [P, P], F32)
+        make_identity(nc, ident_bf[:])
+
+        vs = kept("vs", [P, CHUNKS, PACK], F32)
+        gt_raw = kept("gt_raw", [P, CHUNKS, PACK], BF16)
+        vb = {}
+        raw = {}
+
+        def load(name, x, c, width, dtype):
+            raw[name, c] = kept("%s_raw%d" % (name, c), [P, PACK, width], dtype)
+            nc.sync.dma_start(out=raw[name, c][:], in_=rows(x, c))
+
+        def load_v(c, h):
+            vb[c, h] = kept("vbytes%d%d" % (c, h), [P, PACK, HALF], U8)
+            nc.sync.dma_start(out=vb[c, h][:], in_=rows(v_bytes, c)[:, :, h * HALF:(h + 1) * HALF])
+
+        nc.scalar.activation(out=ident_f32[:], in_=ident_bf[:], func=ACT.Copy)
+        load("k2", k2, 0, M, BF16)
+        nc.sync.dma_start(out=vs[:], in_=v_scale.rearrange("o (c p t) x -> p (o c) (t x)", p=P, t=PACK))
+        load_v(0, 0)
+        load("k2", k2, 1, M, BF16)
+        load_v(1, 0)
+        nc.sync.dma_start(out=gt_raw[:], in_=gt.rearrange("(c p t) -> p c t", p=P, t=PACK))
+        load("k1", k1, 0, D, BF16)
+        load("q1", q1, 0, D, BF16)
+        load("q2", q2, 0, M, BF16)
+        load("u", u, 0, E, BF16)
+        load_v(0, 1)
+        load_v(1, 1)
+        load("k1", k1, 1, D, BF16)
+        load("q1", q1, 1, D, BF16)
+        load("q2", q2, 1, M, BF16)
+        load("u", u, 1, E, BF16)
+
+        gain = kept("gain", [P, CHUNKS, PACK], F32)
+
+        wide = {}
+        grouped = {}
+        codes = {}
+        scales = {}
+        turned = {}
+        zbank = {}
+        gained = {}
+        held = {}
+
+        def group_tile(key, width):
+            grouped[key] = kept("grouped_" + "".join(str(s) for s in key), [P, width * PACK], BF16)
+            return grouped[key]
+
+        def quantise(key, part=0, parts=1):
+            name = "".join(str(s) for s in key)
+            width = grouped[key].shape[1] // PACK
+            if part == 0:
+                codes[key] = kept("codes_" + name, [P, width], U32)
+                scales[key] = kept("scales_" + name, [P, width], U8)
+            lo, hi = part * width // parts, (part + 1) * width // parts
+            nc.vector.quantize_mx(out=codes[key][:, lo:hi].bitcast(FP8X4), scales=scales[key][:, lo:hi],
+                                  in_=grouped[key][:, lo * PACK:hi * PACK])
+
+        def widen_v(c, n):
+            wide[c, n] = stage.tile([P, PACK, PART], BF16, name="wide%d%d" % (c, n), tag="wide", bufs=8)
+            cols = slice((n % 2) * PART, (n % 2 + 1) * PART)
+            for t in range(PACK):
+                nc.scalar.activation(
+                    out=wide[c, n][:, t, :], in_=vb[c, n // 2][:, t, cols].bitcast(FP8),
+                    func=ACT.Copy, scale=vs[:, c, t:t + 1])
+
+        def v_slot(c, n):
+            if ("v", n) not in grouped:
+                group_tile(("v", n), CHUNKS * PART)
+            return grouped["v", n][:, c * PART * PACK:(c + 1) * PART * PACK]
+
+        def interleave_v(c, n):
+            nc.vector.tensor_copy(
+                out=v_slot(c, n).rearrange("p (e i t) -> p e t i", i=4, t=PACK),
+                in_=wide[c, n][:].rearrange("p t (e i) -> p e t i", i=4))
+
+        def weave_v(c, n):
+            b = bank("weave%d%d" % (c, n), [P, 2, HALF], BF16)
+            for s in range(2):
+                nc.tensor.matmul(out=b[:, s, :], lhsT=ident_bf[:],
+                                 rhs=wide[c, n][:, :, s * P:(s + 1) * P].rearrange("p t e -> p e t"), start=True, stop=True)
+            held["weave", c, n] = b
+
+        def take_weave(c, n):
+            nc.scalar.copy(out=v_slot(c, n), in_=held["weave", c, n][:].rearrange("p s e -> p (s e)"))
+            release("weave%d%d" % (c, n))
+
+        def make_gain():
+            nc.vector.tensor_scalar(out=gain[:], in0=gt_raw[:], scalar1=1.0 / D, scalar2=None, op0=ALU.mult)
+
+        def warm(i):
+            b = bank("warm%d" % i, [P, HALF], F32)
+            nc.tensor.matmul(out=b[:], lhsT=ident_bf[:], rhs=raw["k2", 1][:, 0, :], start=True, stop=True)
+            release("warm%d" % i)
+
+        def interleave_k2(c):
+            dst = group_tile(("k2", c), M)
+            nc.vector.tensor_copy(
+                out=dst[:].rearrange("p (s m t) -> p s m t", s=PACK, t=PACK),
+                in_=raw["k2", c][:].rearrange("p t (m s) -> p s m t", s=PACK))
+
+        def turn_qk(name, c):
+            b = bank("tr_%s%d" % (name, c), [P, PACK, P], BF16)
+            for t in range(PACK):
+                nc.tensor.transpose(b[:, t, :], raw[name, c][:, t, :], ident_bf[:])
+            held[name, c] = b
+
+        def take_qk(name, c):
+            turned[name, c] = kept("%sT%d" % (name, c), [P, PACK, P], BF16)
+            nc.scalar.copy(out=turned[name, c][:], in_=held[name, c][:])
+            release("tr_%s%d" % (name, c))
+
+        def scores(c, j):
+            z = bank("z%d%d" % (c, j), [P, PACK, P], F32)
+            for t in range(PACK):
+                nc.tensor.matmul(out=z[:, t, :], lhsT=turned["k1", c][:, t, :], rhs=turned["q1", c][:, j, :], start=True, stop=True)
+            zbank[c, j] = z
+
+        def gain_scores(c, j):
+            z = zbank[c, j]
+            w = stage.tile([P, PACK, P], F32, name="w%d%d" % (c, j), tag="w", bufs=4)
+            for t in range(PACK):
+                nc.scalar.activation(out=w[:, t, :], in_=z[:, t, :], func=ACT.Copy, scale=gain[:, c, t:t + 1])
+            gained[c, j] = w
+
+        def weights(c, j):
+            key = ("a", c, j // 2)
+            if j % 2 == 0:
+                group_tile(key, 2 * P)
+            dst = grouped[key][:, (j % 2) * P * PACK:(j % 2 + 1) * P * PACK]
+            nc.vector.scalar_tensor_tensor(
+                out=dst.rearrange("p (n t) -> p n t", t=PACK),
+                in0=zbank[c, j][:].rearrange("p t n -> p n t"), scalar=0.0,
+                in1=gained[c, j][:].rearrange("p t n -> p n t"), op0=ALU.max, op1=ALU.mult)
+            release("z%d%d" % (c, j))
+
+        def turn_q2(c, pair):
+            b = bank("tr_q2%d%d" % (c, pair), [P, 2, 2, P], F32)
+            words = raw["q2", c][:].rearrange("p t m -> p (t m)").bitcast(F32)
+            for jj in range(2):
+                base = (2 * pair + jj) * (M // 2)
+                for s in range(2):
+                    nc.tensor.transpose(b[:, jj, s, :], words[:, base + s:base + M // 2:2], ident_f32[:])
+            held["q2", c, pair] = b
+
+        def take_q2(c, pair):
+            b = held["q2", c, pair]
+            dst = group_tile(("q2", c, pair), 2 * P)
+            nc.scalar.copy(
+                out=dst[:].bitcast(F32).rearrange("p (j n s) -> p j n s", j=2, s=2),
+                in_=b[:].rearrange("p j s n -> p j n s"))
+            release("tr_q2%d%d" % (c, pair))
+
+        def mx(acc, lhs, lhs_cols, rhs, rhs_cols, start, stop):
+            nc.tensor.matmul_mx(
+                out=acc, lhsT=codes[lhs][:, lhs_cols].bitcast(FP8X4), lhsT_scale=scales[lhs][:, lhs_cols],
+                rhs=codes[rhs][:, rhs_cols].bitcast(FP8X4), rhs_scale=scales[rhs][:, rhs_cols], start=start, stop=stop)
+
+        def memory(n, e):
+            b = bank("m%d%d" % (n, e), [P, PACK, P], F32)
+            for s in range(PACK):
+                for c in range(CHUNKS):
+                    cols = slice(c * PART + e * P, c * PART + (e + 1) * P)
+                    mx(b[:, s, :], ("k2", c), slice(s * P, (s + 1) * P), ("v", n), cols, c == 0, c == CHUNKS - 1)
+            held["m", n, e] = b
+
+        def take_memory(n, e):
+            b = held["m", n, e]
+            if e == 0:
+                group_tile(("m", n), PART)
+            dst = grouped["m", n][:, e * P * PACK:(e + 1) * P * PACK]
+            nc.scalar.copy(out=dst.rearrange("p (x s) -> p x s", s=PACK), in_=b[:].rearrange("p s x -> p x s"))
+            release("m%d%d" % (n, e))
+
+        def products(c, pair, n):
+            b = bank("o%d%d%d" % (c, pair, n), [P, 2, PART], F32)
+            for jj in range(2):
+                cols = slice(jj * P, (jj + 1) * P)
+                mx(b[:, jj, :], ("a", c, pair), cols, ("v", n), slice(c * PART, (c + 1) * PART), True, False)
+                mx(b[:, jj, :], ("q2", c, pair), cols, ("m", n), slice(0, PART), False, True)
+            held["o", c, pair, n] = b
+
+        def finish(c, pair, n):
+            b = held["o", c, pair, n]
+            res = stage.tile([P, 2, PART], F32, name="res%d%d%d" % (c, pair, n), tag="res", bufs=8)
+            span = slice(n * PART, (n + 1) * PART)
+            nc.vector.tensor_tensor(out=res[:], in0=b[:], in1=raw["u", c][:, 2 * pair:2 * pair + 2, span], op=ALU.mult)
+            release("o%d%d%d" % (c, pair, n))
+            nc.sync.dma_start(out=rows(out, c)[:, 2 * pair:2 * pair + 2, span], in_=res[:])
+
+        interleave_k2(0)
+        widen_v(0, 0)
+        quantise(("k2", 0))
+        warm(0)
+        interleave_k2(1)
+        widen_v(0, 1)
+        warm(1)
+        widen_v(1, 0)
+        turn_qk("k1", 0)
+        interleave_v(0, 0)
+        quantise(("k2", 1))
+        turn_qk("q1", 0)
+        take_qk("k1", 0)
+        interleave_v(0, 1)
+        take_qk("q1", 0)
+        turn_q2(0, 0)
+        widen_v(1, 1)
+        make_gain()
+        scores(0, 0)
+        interleave_v(1, 0)
+        scores(0, 1)
+        gain_scores(0, 0)
+        scores(0, 2)
+        interleave_v(1, 1)
+        scores(0, 3)
+        turn_q2(0, 1)
+        take_q2(0, 0)
+        quantise(("v", 0))
+        gain_scores(0, 1)
+        quantise(("v", 1))
+        memory(0, 0)
+        gain_scores(0, 2)
+        weights(0, 0)
+        memory(0, 1)
+        take_memory(0, 0)
+        weights(0, 1)
+        memory(1, 0)
+        take_memory(0, 1)
+        quantise(("q2", 0, 0))
+        memory(1, 1)
+        quantise(("a", 0, 0))
+        gain_scores(0, 3)
+        weights(0, 2)
+        turn_qk("k1", 1)
+        take_q2(0, 1)
+        turn_qk("q1", 1)
+        quantise(("m", 0))
+        turn_q2(1, 0)
+        weights(0, 3)
+        take_memory(1, 0)
+        products(0, 0, 0)
+        quantise(("q2", 0, 1))
+        take_memory(1, 1)
+        quantise(("a", 0, 1))
+        widen_v(0, 2)
+        quantise(("m", 1))
+        finish(0, 0, 0)
+        products(0, 0, 1)
+        take_qk("k1", 1)
+        products(0, 1, 0)
+        interleave_v(0, 2)
+        take_qk("q1", 1)
+        widen_v(1, 2)
+        products(0, 1, 1)
+        finish(0, 0, 1)
+        scores(1, 0)
+        finish(0, 1, 0)
+        scores(1, 1)
+        widen_v(0, 3)
+        interleave_v(1, 2)
+        finish(0, 1, 1)
+        gain_scores(1, 0)
+        quantise(("v", 2))
+        widen_v(1, 3)
+        weights(1, 0)
+        memory(2, 0)
+        interleave_v(0, 3)
+        memory(2, 1)
+        gain_scores(1, 1)
+        interleave_v(1, 3)
+        scores(1, 2)
+        take_q2(1, 0)
+        scores(1, 3)
+        weights(1, 1)
+        turn_q2(1, 1)
+        take_memory(2, 0)
+        quantise(("v", 3))
+        take_memory(2, 1)
+        quantise(("q2", 1, 0))
+        gain_scores(1, 2)
+        quantise(("a", 1, 0))
+        quantise(("m", 2))
+        products(1, 0, 0)
+        gain_scores(1, 3)
+        weights(1, 2)
+        products(1, 0, 1)
+        take_q2(1, 1)
+        finish(1, 0, 0)
+        memory(3, 0)
+        weights(1, 3)
+        memory(3, 1)
+        finish(1, 0, 1)
+        take_memory(3, 0)
+        products(0, 0, 2)
+        quantise(("q2", 1, 1))
+        take_memory(3, 1)
+        products(0, 1, 2)
+        finish(0, 0, 2)
+        products(1, 0, 2)
+        quantise(("a", 1, 1))
+        finish(0, 1, 2)
+        products(1, 1, 0)
+        quantise(("m", 3))
+        products(1, 1, 1)
+        finish(1, 0, 2)
+        products(1, 1, 2)
+        finish(1, 1, 0)
+        products(0, 0, 3)
+        finish(1, 1, 1)
+        products(0, 1, 3)
+        finish(1, 1, 2)
+        products(1, 0, 3)
+        finish(0, 0, 3)
+        products(1, 1, 3)
+        finish(0, 1, 3)
+        finish(1, 0, 3)
+        finish(1, 1, 3)

@@ -20,8 +20,7 @@ PACK = 4
 HALF = 512
 CHUNKS = T // C
 HALVES = E // HALF
-PART = 256
-PARTS = E // PART
+BANKS = 8
 
 
 def tile_flashmixedchunkrelusquaredplusgloballine_kernel(tc, q1, k1, q2, k2, v_bytes, v_scale, gt, u, out):
@@ -32,339 +31,308 @@ def tile_flashmixedchunkrelusquaredplusgloballine_kernel(tc, q1, k1, q2, k2, v_b
 
     with ExitStack() as ctx:
         keep = ctx.enter_context(tc.tile_pool(name="keep", bufs=1))
-        stage = ctx.enter_context(tc.tile_pool(name="stage", bufs=2))
+        stage = ctx.enter_context(tc.tile_pool(name="stage", bufs=8))
         psum = ctx.enter_context(tc.psum_pool(name="psum", bufs=1))
         ctx.enter_context(tc.manual_schedule())
 
-        free_banks = list(range(8))
-        owner = {}
+        free_banks = list(range(BANKS))
+        bank_of = {}
+        in_psum = {}
 
-        def kept(name, shape, dtype):
-            return keep.tile(shape, dtype, name=name, align_bytes=64)
+        def label(key):
+            return "_".join(str(s) for s in key)
 
-        def bank(name, shape, dtype):
-            owner[name] = free_banks.pop(0)
-            return psum.tile(shape, dtype, name=name, tag="bank%d" % owner[name])
+        def kept(key, shape, dtype):
+            return keep.tile(shape, dtype, name=label(key), align_bytes=64)
 
-        def release(name):
-            free_banks.append(owner[name])
+        def take_bank(key, shape, dtype):
+            bank_of[key] = free_banks.pop(0)
+            in_psum[key] = psum.tile(shape, dtype, name=label(key), tag="bank%d" % bank_of[key])
+            return in_psum[key]
 
-        ident_bf = kept("ident_bf", [P, P], BF16)
-        ident_f32 = kept("ident_f32", [P, P], F32)
+        def free_bank(key):
+            free_banks.append(bank_of[key])
+
+        ident_bf = kept(("ident_bf",), [P, P], BF16)
+        ident_f32 = kept(("ident_f32",), [P, P], F32)
         make_identity(nc, ident_bf[:])
+        nc.scalar.activation(out=ident_f32[:], in_=ident_bf[:], func=ACT.Copy)
 
-        vs = kept("vs", [P, CHUNKS, PACK], F32)
-        gt_raw = kept("gt_raw", [P, CHUNKS, PACK], BF16)
+        vs = kept(("vs",), [P, CHUNKS, PACK], F32)
+        gt_raw = kept(("gt_raw",), [P, CHUNKS, PACK], BF16)
+        gain = kept(("gain",), [P, CHUNKS, PACK], F32)
         vb = {}
         raw = {}
 
-        def load(name, x, c, width, dtype):
-            raw[name, c] = kept("%s_raw%d" % (name, c), [P, PACK, width], dtype)
+        def load(name, x, c, width):
+            raw[name, c] = kept(("raw", name, c), [P, PACK, width], BF16)
             nc.sync.dma_start(out=raw[name, c][:], in_=rows(x, c))
 
         def load_v(c, h):
-            vb[c, h] = kept("vbytes%d%d" % (c, h), [P, PACK, HALF], U8)
+            vb[c, h] = kept(("vbytes", c, h), [P, PACK, HALF], U8)
             nc.sync.dma_start(out=vb[c, h][:], in_=rows(v_bytes, c)[:, :, h * HALF:(h + 1) * HALF])
 
-        nc.scalar.activation(out=ident_f32[:], in_=ident_bf[:], func=ACT.Copy)
-        load("k2", k2, 0, M, BF16)
         nc.sync.dma_start(out=vs[:], in_=v_scale.rearrange("o (c p t) x -> p (o c) (t x)", p=P, t=PACK))
         load_v(0, 0)
-        load("k2", k2, 1, M, BF16)
         load_v(1, 0)
-        nc.sync.dma_start(out=gt_raw[:], in_=gt.rearrange("(c p t) -> p c t", p=P, t=PACK))
-        load("k1", k1, 0, D, BF16)
-        load("q1", q1, 0, D, BF16)
-        load("q2", q2, 0, M, BF16)
-        load("u", u, 0, E, BF16)
+        load("k2", k2, 0, M)
+        load("k2", k2, 1, M)
         load_v(0, 1)
+        nc.sync.dma_start(out=gt_raw[:], in_=gt.rearrange("(c p t) -> p c t", p=P, t=PACK))
+        load("k1", k1, 0, D)
+        load("q1", q1, 0, D)
         load_v(1, 1)
-        load("k1", k1, 1, D, BF16)
-        load("q1", q1, 1, D, BF16)
-        load("q2", q2, 1, M, BF16)
-        load("u", u, 1, E, BF16)
-
-        gain = kept("gain", [P, CHUNKS, PACK], F32)
+        load("q2", q2, 0, M)
+        load("k1", k1, 1, D)
+        load("q1", q1, 1, D)
+        load("u", u, 0, E)
+        load("q2", q2, 1, M)
+        load("u", u, 1, E)
 
         wide = {}
         grouped = {}
         codes = {}
         scales = {}
         turned = {}
-        zbank = {}
-        gained = {}
-        held = {}
+        relu = {}
+        squared = {}
+        for c in range(CHUNKS):
+            grouped["k2", c] = kept(("grouped_k2", c), [P, M * PACK], BF16)
+            for h in range(HALVES):
+                wide[c, h] = kept(("wide", c, h), [P, PACK, HALF], BF16)
+                grouped["v", c, h] = kept(("grouped_v", c, h), [P, HALF * PACK], BF16)
+            for pair in range(2):
+                grouped["aq", c, pair] = kept(("grouped_aq", c, pair), [P, 4 * P * PACK], BF16)
+                relu[c, pair] = kept(("relu", c, pair), [P, 2, P * PACK], F32)
+                squared[c, pair] = kept(("squared", c, pair), [P, 2, P * PACK], F32)
+        for h in range(HALVES):
+            grouped["m", h] = kept(("grouped_m", h), [P, HALF * PACK], BF16)
 
-        def group_tile(key, width):
-            grouped[key] = kept("grouped_" + "".join(str(s) for s in key), [P, width * PACK], BF16)
-            return grouped[key]
+        def quantise(*key):
+            codes[key] = kept(("codes",) + key, [P, HALF], U32)
+            scales[key] = kept(("scales",) + key, [P, HALF], U8)
+            nc.vector.quantize_mx(out=codes[key][:].bitcast(FP8X4), scales=scales[key][:], in_=grouped[key][:])
 
-        def quantise(key, part=0, parts=1):
-            name = "".join(str(s) for s in key)
-            width = grouped[key].shape[1] // PACK
-            if part == 0:
-                codes[key] = kept("codes_" + name, [P, width], U32)
-                scales[key] = kept("scales_" + name, [P, width], U8)
-            lo, hi = part * width // parts, (part + 1) * width // parts
-            nc.vector.quantize_mx(out=codes[key][:, lo:hi].bitcast(FP8X4), scales=scales[key][:, lo:hi],
-                                  in_=grouped[key][:, lo * PACK:hi * PACK])
+        def widen_scalar(c, h, planes):
+            for t in planes:
+                nc.scalar.activation(out=wide[c, h][:, t, :], in_=vb[c, h][:, t, :].bitcast(FP8),
+                                     func=ACT.Copy, scale=vs[:, c, t:t + 1])
 
-        def widen_v(c, n):
-            wide[c, n] = stage.tile([P, PACK, PART], BF16, name="wide%d%d" % (c, n), tag="wide", bufs=8)
-            cols = slice((n % 2) * PART, (n % 2 + 1) * PART)
-            for t in range(PACK):
-                nc.scalar.activation(
-                    out=wide[c, n][:, t, :], in_=vb[c, n // 2][:, t, cols].bitcast(FP8),
-                    func=ACT.Copy, scale=vs[:, c, t:t + 1])
+        def widen_vector(c, h, planes):
+            for t in planes:
+                nc.vector.tensor_scalar(out=wide[c, h][:, t, :], in0=vb[c, h][:, t, :].bitcast(FP8),
+                                        scalar1=vs[:, c, t:t + 1], scalar2=None, op0=ALU.mult)
 
-        def v_slot(c, n):
-            if ("v", n) not in grouped:
-                group_tile(("v", n), CHUNKS * PART)
-            return grouped["v", n][:, c * PART * PACK:(c + 1) * PART * PACK]
+        def interleave_v(copy, c, h, lo, hi):
+            copy(out=grouped["v", c, h][:, lo * PACK:hi * PACK].rearrange("p (e i t) -> p e t i", i=4, t=PACK),
+                 in_=wide[c, h][:, :, lo:hi].rearrange("p t (e i) -> p e t i", i=4))
 
-        def interleave_v(c, n):
+        def interleave_k2(c):
             nc.vector.tensor_copy(
-                out=v_slot(c, n).rearrange("p (e i t) -> p e t i", i=4, t=PACK),
-                in_=wide[c, n][:].rearrange("p t (e i) -> p e t i", i=4))
-
-        def weave_v(c, n):
-            b = bank("weave%d%d" % (c, n), [P, 2, HALF], BF16)
-            for s in range(2):
-                nc.tensor.matmul(out=b[:, s, :], lhsT=ident_bf[:],
-                                 rhs=wide[c, n][:, :, s * P:(s + 1) * P].rearrange("p t e -> p e t"), start=True, stop=True)
-            held["weave", c, n] = b
-
-        def take_weave(c, n):
-            nc.scalar.copy(out=v_slot(c, n), in_=held["weave", c, n][:].rearrange("p s e -> p (s e)"))
-            release("weave%d%d" % (c, n))
+                out=grouped["k2", c][:].rearrange("p (s b i t) -> p b s i t", s=PACK, i=2, t=PACK),
+                in_=raw["k2", c][:].rearrange("p t (b i s) -> p b s i t", i=2, s=PACK))
 
         def make_gain():
             nc.vector.tensor_scalar(out=gain[:], in0=gt_raw[:], scalar1=1.0 / D, scalar2=None, op0=ALU.mult)
 
-        def warm(i):
-            b = bank("warm%d" % i, [P, HALF], F32)
+        def warm_up(i):
+            b = take_bank(("warm", i), [P, HALF], F32)
             nc.tensor.matmul(out=b[:], lhsT=ident_bf[:], rhs=raw["k2", 1][:, 0, :], start=True, stop=True)
-            release("warm%d" % i)
+            free_bank(("warm", i))
 
-        def interleave_k2(c):
-            dst = group_tile(("k2", c), M)
-            nc.vector.tensor_copy(
-                out=dst[:].rearrange("p (s m t) -> p s m t", s=PACK, t=PACK),
-                in_=raw["k2", c][:].rearrange("p t (m s) -> p s m t", s=PACK))
-
-        def turn_qk(name, c):
-            b = bank("tr_%s%d" % (name, c), [P, PACK, P], BF16)
+        def turn(name, c):
+            b = take_bank(("turn", name, c), [P, PACK, P], BF16)
             for t in range(PACK):
                 nc.tensor.transpose(b[:, t, :], raw[name, c][:, t, :], ident_bf[:])
-            held[name, c] = b
 
-        def take_qk(name, c):
-            turned[name, c] = kept("%sT%d" % (name, c), [P, PACK, P], BF16)
-            nc.scalar.copy(out=turned[name, c][:], in_=held[name, c][:])
-            release("tr_%s%d" % (name, c))
+        def take_turned(name, c):
+            turned[name, c] = kept(("turned", name, c), [P, PACK, P], BF16)
+            nc.scalar.copy(out=turned[name, c][:], in_=in_psum["turn", name, c][:])
+            free_bank(("turn", name, c))
 
         def scores(c, j):
-            z = bank("z%d%d" % (c, j), [P, PACK, P], F32)
+            z = take_bank(("z", c, j), [P, PACK, P], F32)
             for t in range(PACK):
-                nc.tensor.matmul(out=z[:, t, :], lhsT=turned["k1", c][:, t, :], rhs=turned["q1", c][:, j, :], start=True, stop=True)
-            zbank[c, j] = z
+                nc.tensor.matmul(out=z[:, t, :], lhsT=turned["k1", c][:, t, :], rhs=turned["q1", c][:, j, :],
+                                 start=True, stop=True)
 
-        def gain_scores(c, j):
-            z = zbank[c, j]
-            w = stage.tile([P, PACK, P], F32, name="w%d%d" % (c, j), tag="w", bufs=4)
-            for t in range(PACK):
-                nc.scalar.activation(out=w[:, t, :], in_=z[:, t, :], func=ACT.Copy, scale=gain[:, c, t:t + 1])
-            gained[c, j] = w
+        def take_relu(c, j):
+            nc.scalar.activation(out=relu[c, j // 2][:, j % 2, :].rearrange("p (n t) -> p n t", t=PACK),
+                                 in_=in_psum["z", c, j][:].rearrange("p t n -> p n t"), func=ACT.Relu)
+            free_bank(("z", c, j))
+
+        def square(c, j):
+            nc.scalar.activation(out=squared[c, j // 2][:, j % 2, :], in_=relu[c, j // 2][:, j % 2, :], func=ACT.Square)
 
         def weights(c, j):
-            key = ("a", c, j // 2)
-            if j % 2 == 0:
-                group_tile(key, 2 * P)
-            dst = grouped[key][:, (j % 2) * P * PACK:(j % 2 + 1) * P * PACK]
-            nc.vector.scalar_tensor_tensor(
-                out=dst.rearrange("p (n t) -> p n t", t=PACK),
-                in0=zbank[c, j][:].rearrange("p t n -> p n t"), scalar=0.0,
-                in1=gained[c, j][:].rearrange("p t n -> p n t"), op0=ALU.max, op1=ALU.mult)
-            release("z%d%d" % (c, j))
+            nc.vector.tensor_tensor(
+                out=grouped["aq", c, j // 2][:, (j % 2) * P * PACK:(j % 2 + 1) * P * PACK].rearrange("p (n t) -> p n t", t=PACK),
+                in0=squared[c, j // 2][:, j % 2, :].rearrange("p (n t) -> p n t", t=PACK),
+                in1=gain[:, c:c + 1, :].to_broadcast([P, P, PACK]), op=ALU.mult)
 
         def turn_q2(c, pair):
-            b = bank("tr_q2%d%d" % (c, pair), [P, 2, 2, P], F32)
+            b = take_bank(("turn_q2", c, pair), [P, 2, 2, P], F32)
             words = raw["q2", c][:].rearrange("p t m -> p (t m)").bitcast(F32)
             for jj in range(2):
                 base = (2 * pair + jj) * (M // 2)
                 for s in range(2):
                     nc.tensor.transpose(b[:, jj, s, :], words[:, base + s:base + M // 2:2], ident_f32[:])
-            held["q2", c, pair] = b
 
         def take_q2(c, pair):
-            b = held["q2", c, pair]
-            dst = group_tile(("q2", c, pair), 2 * P)
             nc.scalar.copy(
-                out=dst[:].bitcast(F32).rearrange("p (j n s) -> p j n s", j=2, s=2),
-                in_=b[:].rearrange("p j s n -> p j n s"))
-            release("tr_q2%d%d" % (c, pair))
+                out=grouped["aq", c, pair][:, 2 * P * PACK:].bitcast(F32).rearrange("p (j n s) -> p j n s", j=2, s=2),
+                in_=in_psum["turn_q2", c, pair][:].rearrange("p j s n -> p j n s"))
+            free_bank(("turn_q2", c, pair))
 
         def mx(acc, lhs, lhs_cols, rhs, rhs_cols, start, stop):
             nc.tensor.matmul_mx(
                 out=acc, lhsT=codes[lhs][:, lhs_cols].bitcast(FP8X4), lhsT_scale=scales[lhs][:, lhs_cols],
                 rhs=codes[rhs][:, rhs_cols].bitcast(FP8X4), rhs_scale=scales[rhs][:, rhs_cols], start=start, stop=stop)
 
-        def memory(n, e):
-            b = bank("m%d%d" % (n, e), [P, PACK, P], F32)
+        def block(i):
+            return slice(i * P, (i + 1) * P)
+
+        def memory(h, e):
+            b = take_bank(("m", h, e), [P, PACK, P], F32)
             for s in range(PACK):
                 for c in range(CHUNKS):
-                    cols = slice(c * PART + e * P, c * PART + (e + 1) * P)
-                    mx(b[:, s, :], ("k2", c), slice(s * P, (s + 1) * P), ("v", n), cols, c == 0, c == CHUNKS - 1)
-            held["m", n, e] = b
+                    mx(b[:, s, :], ("k2", c), block(s), ("v", c, h), block(e), c == 0, c == CHUNKS - 1)
 
-        def take_memory(n, e):
-            b = held["m", n, e]
-            if e == 0:
-                group_tile(("m", n), PART)
-            dst = grouped["m", n][:, e * P * PACK:(e + 1) * P * PACK]
-            nc.scalar.copy(out=dst.rearrange("p (x s) -> p x s", s=PACK), in_=b[:].rearrange("p s x -> p x s"))
-            release("m%d%d" % (n, e))
+        def take_memory(h, e):
+            dst = grouped["m", h][:, e * P * PACK:(e + 1) * P * PACK]
+            nc.scalar.copy(out=dst.rearrange("p (x s) -> p x s", s=PACK),
+                           in_=in_psum["m", h, e][:].rearrange("p s x -> p x s"))
+            free_bank(("m", h, e))
 
-        def products(c, pair, n):
-            b = bank("o%d%d%d" % (c, pair, n), [P, 2, PART], F32)
-            for jj in range(2):
-                cols = slice(jj * P, (jj + 1) * P)
-                mx(b[:, jj, :], ("a", c, pair), cols, ("v", n), slice(c * PART, (c + 1) * PART), True, False)
-                mx(b[:, jj, :], ("q2", c, pair), cols, ("m", n), slice(0, PART), False, True)
-            held["o", c, pair, n] = b
+        def products(c, j, h):
+            b = take_bank(("o", c, j, h), [P, HALF], F32)
+            mx(b[:], ("aq", c, j // 2), block(j % 2), ("v", c, h), slice(0, HALF), True, False)
+            mx(b[:], ("aq", c, j // 2), block(2 + j % 2), ("m", h), slice(0, HALF), False, True)
 
-        def finish(c, pair, n):
-            b = held["o", c, pair, n]
-            res = stage.tile([P, 2, PART], F32, name="res%d%d%d" % (c, pair, n), tag="res", bufs=8)
-            span = slice(n * PART, (n + 1) * PART)
-            nc.vector.tensor_tensor(out=res[:], in0=b[:], in1=raw["u", c][:, 2 * pair:2 * pair + 2, span], op=ALU.mult)
-            release("o%d%d%d" % (c, pair, n))
-            nc.sync.dma_start(out=rows(out, c)[:, 2 * pair:2 * pair + 2, span], in_=res[:])
+        def finish(c, j, h):
+            res = stage.tile([P, HALF], F32, name=label(("res", c, j, h)), tag="res")
+            span = slice(h * HALF, (h + 1) * HALF)
+            nc.vector.tensor_tensor(out=res[:], in0=in_psum["o", c, j, h][:], in1=raw["u", c][:, j, span], op=ALU.mult)
+            free_bank(("o", c, j, h))
+            nc.sync.dma_start(out=rows(out, c)[:, j, span], in_=res[:])
 
+        widen_vector(0, 0, (0, 1, 2))
+        widen_scalar(0, 0, (3,))
+        widen_scalar(1, 0, (0, 1, 2, 3))
+        interleave_v(nc.vector.tensor_copy, 0, 0, 0, HALF)
         interleave_k2(0)
-        widen_v(0, 0)
-        quantise(("k2", 0))
-        warm(0)
+        warm_up(0)
+        interleave_v(nc.scalar.copy, 1, 0, HALF // 2, HALF)
         interleave_k2(1)
-        widen_v(0, 1)
-        warm(1)
-        widen_v(1, 0)
-        turn_qk("k1", 0)
-        interleave_v(0, 0)
-        quantise(("k2", 1))
-        turn_qk("q1", 0)
-        take_qk("k1", 0)
-        interleave_v(0, 1)
-        take_qk("q1", 0)
-        turn_q2(0, 0)
-        widen_v(1, 1)
-        make_gain()
+        turn("k1", 0)
+        turn("q1", 0)
+        warm_up(1)
+        widen_scalar(0, 1, (0, 1))
+        interleave_v(nc.vector.tensor_copy, 1, 0, 0, HALF // 2)
+        quantise("k2", 0)
+        take_turned("k1", 0)
+        take_turned("q1", 0)
+        quantise("v", 0, 0)
+        widen_scalar(1, 1, (0, 1))
         scores(0, 0)
-        interleave_v(1, 0)
         scores(0, 1)
-        gain_scores(0, 0)
-        scores(0, 2)
-        interleave_v(1, 1)
-        scores(0, 3)
-        turn_q2(0, 1)
-        take_q2(0, 0)
-        quantise(("v", 0))
-        gain_scores(0, 1)
-        quantise(("v", 1))
+        quantise("k2", 1)
+        quantise("v", 1, 0)
+        turn_q2(0, 0)
+        widen_vector(0, 1, (2, 3))
+        widen_vector(1, 1, (2, 3))
+        take_relu(0, 0)
+        take_relu(0, 1)
         memory(0, 0)
-        gain_scores(0, 2)
-        weights(0, 0)
         memory(0, 1)
+        turn("k1", 1)
+        turn("q1", 1)
+        square(0, 0)
+        square(0, 1)
+        interleave_v(nc.vector.tensor_copy, 0, 1, 0, HALF)
+        take_q2(0, 0)
+        scores(0, 2)
+        scores(0, 3)
         take_memory(0, 0)
-        weights(0, 1)
-        memory(1, 0)
         take_memory(0, 1)
-        quantise(("q2", 0, 0))
-        memory(1, 1)
-        quantise(("a", 0, 0))
-        gain_scores(0, 3)
-        weights(0, 2)
-        turn_qk("k1", 1)
-        take_q2(0, 1)
-        turn_qk("q1", 1)
-        quantise(("m", 0))
-        turn_q2(1, 0)
-        weights(0, 3)
-        take_memory(1, 0)
-        products(0, 0, 0)
-        quantise(("q2", 0, 1))
-        take_memory(1, 1)
-        quantise(("a", 0, 1))
-        widen_v(0, 2)
-        quantise(("m", 1))
-        finish(0, 0, 0)
-        products(0, 0, 1)
-        take_qk("k1", 1)
-        products(0, 1, 0)
-        interleave_v(0, 2)
-        take_qk("q1", 1)
-        widen_v(1, 2)
-        products(0, 1, 1)
-        finish(0, 0, 1)
+        memory(0, 2)
+        memory(0, 3)
+        interleave_v(nc.vector.tensor_copy, 1, 1, 0, HALF)
+        take_turned("k1", 1)
+        take_turned("q1", 1)
+        turn_q2(0, 1)
+        make_gain()
+        quantise("v", 0, 1)
+        weights(0, 0)
+        take_relu(0, 2)
+        square(0, 2)
+        quantise("v", 1, 1)
+        weights(0, 1)
+        take_memory(0, 2)
+        take_memory(0, 3)
         scores(1, 0)
-        finish(0, 1, 0)
         scores(1, 1)
-        widen_v(0, 3)
-        interleave_v(1, 2)
-        finish(0, 1, 1)
-        gain_scores(1, 0)
-        quantise(("v", 2))
-        widen_v(1, 3)
+        take_relu(0, 3)
+        square(0, 3)
+        weights(0, 2)
+        quantise("aq", 0, 0)
+        quantise("m", 0)
+        memory(1, 0)
+        memory(1, 1)
+        take_q2(0, 1)
+        weights(0, 3)
+        products(0, 0, 0)
+        products(0, 1, 0)
+        take_relu(1, 0)
+        square(1, 0)
+        memory(1, 2)
+        finish(0, 0, 0)
+        quantise("aq", 0, 1)
+        take_memory(1, 0)
+        take_memory(1, 1)
+        memory(1, 3)
+        finish(0, 1, 0)
         weights(1, 0)
-        memory(2, 0)
-        interleave_v(0, 3)
-        memory(2, 1)
-        gain_scores(1, 1)
-        interleave_v(1, 3)
+        products(0, 2, 0)
+        products(0, 3, 0)
+        turn_q2(1, 0)
+        take_memory(1, 2)
+        take_memory(1, 3)
+        finish(0, 2, 0)
+        finish(0, 3, 0)
+        take_relu(1, 1)
+        square(1, 1)
         scores(1, 2)
-        take_q2(1, 0)
         scores(1, 3)
+        quantise("m", 1)
+        take_q2(1, 0)
         weights(1, 1)
+        products(0, 0, 1)
+        products(0, 1, 1)
         turn_q2(1, 1)
-        take_memory(2, 0)
-        quantise(("v", 3))
-        take_memory(2, 1)
-        quantise(("q2", 1, 0))
-        gain_scores(1, 2)
-        quantise(("a", 1, 0))
-        quantise(("m", 2))
-        products(1, 0, 0)
-        gain_scores(1, 3)
-        weights(1, 2)
-        products(1, 0, 1)
+        take_relu(1, 2)
+        square(1, 2)
+        finish(0, 0, 1)
+        quantise("aq", 1, 0)
+        products(0, 2, 1)
+        products(0, 3, 1)
+        finish(0, 1, 1)
+        take_relu(1, 3)
+        square(1, 3)
         take_q2(1, 1)
-        finish(1, 0, 0)
-        memory(3, 0)
+        weights(1, 2)
+        products(1, 0, 0)
+        products(1, 0, 1)
+        finish(0, 2, 1)
         weights(1, 3)
-        memory(3, 1)
-        finish(1, 0, 1)
-        take_memory(3, 0)
-        products(0, 0, 2)
-        quantise(("q2", 1, 1))
-        take_memory(3, 1)
-        products(0, 1, 2)
-        finish(0, 0, 2)
-        products(1, 0, 2)
-        quantise(("a", 1, 1))
-        finish(0, 1, 2)
         products(1, 1, 0)
-        quantise(("m", 3))
         products(1, 1, 1)
-        finish(1, 0, 2)
-        products(1, 1, 2)
-        finish(1, 1, 0)
-        products(0, 0, 3)
-        finish(1, 1, 1)
-        products(0, 1, 3)
-        finish(1, 1, 2)
-        products(1, 0, 3)
-        finish(0, 0, 3)
-        products(1, 1, 3)
-        finish(0, 1, 3)
-        finish(1, 0, 3)
-        finish(1, 1, 3)
+        finish(0, 3, 1)
+        quantise("aq", 1, 1)
+        for j in range(2):
+            for h in range(HALVES):
+                finish(1, j, h)
+                products(1, 2 + j, h)
+        for j in range(2, 4):
+            for h in range(HALVES):
+                finish(1, j, h)

@@ -56,7 +56,6 @@ def tile_flashmixedchunkrelusquaredplusgloballine_kernel(tc, q1, k1, q2, k2, v_b
         ident_bf = kept(("ident_bf",), [P, P], BF16)
         ident_f32 = kept(("ident_f32",), [P, P], F32)
         make_identity(nc, ident_bf[:])
-        nc.scalar.activation(out=ident_f32[:], in_=ident_bf[:], func=ACT.Copy)
 
         vs = kept(("vs",), [P, CHUNKS, PACK], F32)
         gt_raw = kept(("gt_raw",), [P, CHUNKS, PACK], BF16)
@@ -68,20 +67,24 @@ def tile_flashmixedchunkrelusquaredplusgloballine_kernel(tc, q1, k1, q2, k2, v_b
             raw[name, c] = kept(("raw", name, c), [P, PACK, width], BF16)
             nc.sync.dma_start(out=raw[name, c][:], in_=rows(x, c))
 
-        def load_v(c, h):
-            vb[c, h] = kept(("vbytes", c, h), [P, PACK, HALF], U8)
-            nc.sync.dma_start(out=vb[c, h][:], in_=rows(v_bytes, c)[:, :, h * HALF:(h + 1) * HALF])
+        def load_v(c, h, lo, hi):
+            tile = kept(("vbytes", c, h, lo), [P, hi - lo, HALF], U8)
+            nc.sync.dma_start(out=tile[:], in_=rows(v_bytes, c)[:, lo:hi, h * HALF:(h + 1) * HALF])
+            for t in range(lo, hi):
+                vb[c, h, t] = tile[:, t - lo, :]
 
-        nc.sync.dma_start(out=vs[:], in_=v_scale.rearrange("o (c p t) x -> p (o c) (t x)", p=P, t=PACK))
-        load_v(0, 0)
-        load_v(1, 0)
+        nc.scalar.dma_start(out=vs[:], in_=v_scale.rearrange("o (c p t) x -> p (o c) (t x)", p=P, t=PACK))
+        nc.scalar.activation(out=ident_f32[:], in_=ident_bf[:], func=ACT.Copy)
+        load_v(0, 0, 0, 2)
+        load_v(0, 0, 2, PACK)
+        load_v(1, 0, 0, PACK)
         load("k2", k2, 0, M)
         load("k2", k2, 1, M)
-        load_v(0, 1)
-        nc.sync.dma_start(out=gt_raw[:], in_=gt.rearrange("(c p t) -> p c t", p=P, t=PACK))
         load("k1", k1, 0, D)
         load("q1", q1, 0, D)
-        load_v(1, 1)
+        load_v(0, 1, 0, PACK)
+        nc.sync.dma_start(out=gt_raw[:], in_=gt.rearrange("(c p t) -> p c t", p=P, t=PACK))
+        load_v(1, 1, 0, PACK)
         load("q2", q2, 0, M)
         load("k1", k1, 1, D)
         load("q1", q1, 1, D)
@@ -97,39 +100,45 @@ def tile_flashmixedchunkrelusquaredplusgloballine_kernel(tc, q1, k1, q2, k2, v_b
         relu = {}
         squared = {}
         for c in range(CHUNKS):
-            grouped["k2", c] = kept(("grouped_k2", c), [P, M * PACK], BF16)
             for h in range(HALVES):
                 wide[c, h] = kept(("wide", c, h), [P, PACK, HALF], BF16)
-                grouped["v", c, h] = kept(("grouped_v", c, h), [P, HALF * PACK], BF16)
             for pair in range(2):
                 grouped["aq", c, pair] = kept(("grouped_aq", c, pair), [P, 4 * P * PACK], BF16)
                 relu[c, pair] = kept(("relu", c, pair), [P, 2, P * PACK], F32)
                 squared[c, pair] = kept(("squared", c, pair), [P, 2, P * PACK], F32)
         for h in range(HALVES):
             grouped["m", h] = kept(("grouped_m", h), [P, HALF * PACK], BF16)
+            grouped["v", h] = kept(("grouped_v", h), [P, CHUNKS * HALF * PACK], BF16)
+        grouped["k2",] = kept(("grouped_k2",), [P, CHUNKS * M * PACK], BF16)
+
+        for key in grouped:
+            codes[key] = kept(("codes",) + key, [P, grouped[key].shape[1] // PACK], U32)
+            scales[key] = kept(("scales",) + key, [P, grouped[key].shape[1] // PACK], U8)
+
+        def quantise_columns(key, lo, hi):
+            nc.vector.quantize_mx(out=codes[key][:, lo:hi].bitcast(FP8X4), scales=scales[key][:, lo:hi],
+                                  in_=grouped[key][:, lo * PACK:hi * PACK])
 
         def quantise(*key):
-            codes[key] = kept(("codes",) + key, [P, HALF], U32)
-            scales[key] = kept(("scales",) + key, [P, HALF], U8)
-            nc.vector.quantize_mx(out=codes[key][:].bitcast(FP8X4), scales=scales[key][:], in_=grouped[key][:])
+            quantise_columns(key, 0, codes[key].shape[1])
 
         def widen_scalar(c, h, planes):
             for t in planes:
-                nc.scalar.activation(out=wide[c, h][:, t, :], in_=vb[c, h][:, t, :].bitcast(FP8),
+                nc.scalar.activation(out=wide[c, h][:, t, :], in_=vb[c, h, t].bitcast(FP8),
                                      func=ACT.Copy, scale=vs[:, c, t:t + 1])
 
         def widen_vector(c, h, planes):
             for t in planes:
-                nc.vector.tensor_scalar(out=wide[c, h][:, t, :], in0=vb[c, h][:, t, :].bitcast(FP8),
+                nc.vector.tensor_scalar(out=wide[c, h][:, t, :], in0=vb[c, h, t].bitcast(FP8),
                                         scalar1=vs[:, c, t:t + 1], scalar2=None, op0=ALU.mult)
 
         def interleave_v(copy, c, h, lo, hi):
-            copy(out=grouped["v", c, h][:, lo * PACK:hi * PACK].rearrange("p (e i t) -> p e t i", i=4, t=PACK),
+            copy(out=grouped["v", h][:, (c * HALF + lo) * PACK:(c * HALF + hi) * PACK].rearrange("p (e i t) -> p e t i", i=4, t=PACK),
                  in_=wide[c, h][:, :, lo:hi].rearrange("p t (e i) -> p e t i", i=4))
 
         def interleave_k2(c):
             nc.vector.tensor_copy(
-                out=grouped["k2", c][:].rearrange("p (s b i t) -> p b s i t", s=PACK, i=2, t=PACK),
+                out=grouped["k2",][:, c * M * PACK:(c + 1) * M * PACK].rearrange("p (s b i t) -> p b s i t", s=PACK, i=2, t=PACK),
                 in_=raw["k2", c][:].rearrange("p t (b i s) -> p b s i t", i=2, s=PACK))
 
         def make_gain():
@@ -137,7 +146,7 @@ def tile_flashmixedchunkrelusquaredplusgloballine_kernel(tc, q1, k1, q2, k2, v_b
 
         def warm_up(i):
             b = take_bank(("warm", i), [P, HALF], F32)
-            nc.tensor.matmul(out=b[:], lhsT=ident_bf[:], rhs=raw["k2", 1][:, 0, :], start=True, stop=True)
+            nc.tensor.matmul(out=b[:], lhsT=ident_bf[:], rhs=raw["k2", 0][:, 0, :], start=True, stop=True)
             free_bank(("warm", i))
 
         def turn(name, c):
@@ -161,14 +170,15 @@ def tile_flashmixedchunkrelusquaredplusgloballine_kernel(tc, q1, k1, q2, k2, v_b
                                  in_=in_psum["z", c, j][:].rearrange("p t n -> p n t"), func=ACT.Relu)
             free_bank(("z", c, j))
 
-        def square(c, j):
-            nc.scalar.activation(out=squared[c, j // 2][:, j % 2, :], in_=relu[c, j // 2][:, j % 2, :], func=ACT.Square)
+        def square(c, pair, lo=0, hi=2):
+            nc.scalar.activation(out=squared[c, pair][:, lo:hi, :], in_=relu[c, pair][:, lo:hi, :], func=ACT.Square)
 
-        def weights(c, j):
+        def weights(c, pair, lo=0, hi=2):
+            dst = grouped["aq", c, pair][:].rearrange("p (x j n t) -> p x j n t", j=2, x=2, t=PACK)
             nc.vector.tensor_tensor(
-                out=grouped["aq", c, j // 2][:, (j % 2) * P * PACK:(j % 2 + 1) * P * PACK].rearrange("p (n t) -> p n t", t=PACK),
-                in0=squared[c, j // 2][:, j % 2, :].rearrange("p (n t) -> p n t", t=PACK),
-                in1=gain[:, c:c + 1, :].to_broadcast([P, P, PACK]), op=ALU.mult)
+                out=dst[:, 0, lo:hi, :, :],
+                in0=squared[c, pair][:, lo:hi, :].rearrange("p j (n t) -> p j n t", t=PACK),
+                in1=gain[:, c:c + 1, :].unsqueeze(1).to_broadcast([P, hi - lo, P, PACK]), op=ALU.mult)
 
         def turn_q2(c, pair):
             b = take_bank(("turn_q2", c, pair), [P, 2, 2, P], F32)
@@ -196,7 +206,7 @@ def tile_flashmixedchunkrelusquaredplusgloballine_kernel(tc, q1, k1, q2, k2, v_b
             b = take_bank(("m", h, e), [P, PACK, P], F32)
             for s in range(PACK):
                 for c in range(CHUNKS):
-                    mx(b[:, s, :], ("k2", c), block(s), ("v", c, h), block(e), c == 0, c == CHUNKS - 1)
+                    mx(b[:, s, :], ("k2",), block(PACK * c + s), ("v", h), block(PACK * c + e), c == 0, c == CHUNKS - 1)
 
         def take_memory(h, e):
             dst = grouped["m", h][:, e * P * PACK:(e + 1) * P * PACK]
@@ -206,15 +216,18 @@ def tile_flashmixedchunkrelusquaredplusgloballine_kernel(tc, q1, k1, q2, k2, v_b
 
         def products(c, j, h):
             b = take_bank(("o", c, j, h), [P, HALF], F32)
-            mx(b[:], ("aq", c, j // 2), block(j % 2), ("v", c, h), slice(0, HALF), True, False)
+            mx(b[:], ("aq", c, j // 2), block(j % 2), ("v", h), slice(c * HALF, (c + 1) * HALF), True, False)
             mx(b[:], ("aq", c, j // 2), block(2 + j % 2), ("m", h), slice(0, HALF), False, True)
 
-        def finish(c, j, h):
-            res = stage.tile([P, HALF], F32, name=label(("res", c, j, h)), tag="res")
-            span = slice(h * HALF, (h + 1) * HALF)
-            nc.vector.tensor_tensor(out=res[:], in0=in_psum["o", c, j, h][:], in1=raw["u", c][:, j, span], op=ALU.mult)
+        def finish(c, j, h, parts=1):
+            width = HALF // parts
+            for part in range(parts):
+                res = stage.tile([P, width], F32, name=label(("res", c, j, h, part)), tag="res")
+                span = slice(h * HALF + part * width, h * HALF + (part + 1) * width)
+                nc.vector.tensor_tensor(out=res[:], in0=in_psum["o", c, j, h][:, part * width:(part + 1) * width],
+                                        in1=raw["u", c][:, j, span], op=ALU.mult)
+                nc.sync.dma_start(out=rows(out, c)[:, j, span], in_=res[:])
             free_bank(("o", c, j, h))
-            nc.sync.dma_start(out=rows(out, c)[:, j, span], in_=res[:])
 
         widen_vector(0, 0, (0, 1, 2))
         widen_scalar(0, 0, (3,))
@@ -222,117 +235,106 @@ def tile_flashmixedchunkrelusquaredplusgloballine_kernel(tc, q1, k1, q2, k2, v_b
         interleave_v(nc.vector.tensor_copy, 0, 0, 0, HALF)
         interleave_k2(0)
         warm_up(0)
+        warm_up(1)
         interleave_v(nc.scalar.copy, 1, 0, HALF // 2, HALF)
         interleave_k2(1)
         turn("k1", 0)
         turn("q1", 0)
-        warm_up(1)
-        widen_scalar(0, 1, (0, 1))
-        interleave_v(nc.vector.tensor_copy, 1, 0, 0, HALF // 2)
-        quantise("k2", 0)
+        warm_up(2)
         take_turned("k1", 0)
+        widen_scalar(0, 1, (0,))
         take_turned("q1", 0)
-        quantise("v", 0, 0)
-        widen_scalar(1, 1, (0, 1))
-        scores(0, 0)
-        scores(0, 1)
-        quantise("k2", 1)
-        quantise("v", 1, 0)
+        widen_scalar(0, 1, (1,))
+        interleave_v(nc.vector.tensor_copy, 1, 0, 0, HALF // 2)
+        quantise("k2")
+        quantise("v", 0)
+        for j in range(4):
+            scores(0, j)
+        widen_scalar(1, 1, (0, 1, 2))
         turn_q2(0, 0)
         widen_vector(0, 1, (2, 3))
-        widen_vector(1, 1, (2, 3))
+        widen_vector(1, 1, (3,))
         take_relu(0, 0)
         take_relu(0, 1)
-        memory(0, 0)
-        memory(0, 1)
         turn("k1", 1)
         turn("q1", 1)
-        square(0, 0)
-        square(0, 1)
-        interleave_v(nc.vector.tensor_copy, 0, 1, 0, HALF)
+        memory(0, 0)
+        memory(0, 1)
         take_q2(0, 0)
-        scores(0, 2)
-        scores(0, 3)
-        take_memory(0, 0)
-        take_memory(0, 1)
+        square(0, 0)
+        interleave_v(nc.vector.tensor_copy, 0, 1, 0, HALF)
+        interleave_v(nc.vector.tensor_copy, 1, 1, 0, HALF)
+        take_relu(0, 2)
+        take_relu(0, 3)
         memory(0, 2)
         memory(0, 3)
-        interleave_v(nc.vector.tensor_copy, 1, 1, 0, HALF)
+        turn_q2(0, 1)
         take_turned("k1", 1)
         take_turned("q1", 1)
-        turn_q2(0, 1)
+        square(0, 1)
         make_gain()
-        quantise("v", 0, 1)
+        quantise("v", 1)
         weights(0, 0)
-        take_relu(0, 2)
-        square(0, 2)
-        quantise("v", 1, 1)
         weights(0, 1)
-        take_memory(0, 2)
-        take_memory(0, 3)
+        for e in range(4):
+            take_memory(0, e)
         scores(1, 0)
         scores(1, 1)
-        take_relu(0, 3)
-        square(0, 3)
-        weights(0, 2)
+        take_q2(0, 1)
+        for e in range(4):
+            memory(1, e)
         quantise("aq", 0, 0)
         quantise("m", 0)
-        memory(1, 0)
-        memory(1, 1)
-        take_q2(0, 1)
-        weights(0, 3)
-        products(0, 0, 0)
-        products(0, 1, 0)
-        take_relu(1, 0)
-        square(1, 0)
-        memory(1, 2)
-        finish(0, 0, 0)
         quantise("aq", 0, 1)
-        take_memory(1, 0)
-        take_memory(1, 1)
-        memory(1, 3)
-        finish(0, 1, 0)
-        weights(1, 0)
-        products(0, 2, 0)
-        products(0, 3, 0)
+        for e in range(4):
+            take_memory(1, e)
+        for j in range(4):
+            products(0, j, 0)
         turn_q2(1, 0)
-        take_memory(1, 2)
-        take_memory(1, 3)
+        take_relu(1, 0)
+        take_relu(1, 1)
+        finish(0, 0, 0)
+        finish(0, 1, 0)
+        quantise("m", 1)
         finish(0, 2, 0)
         finish(0, 3, 0)
-        take_relu(1, 1)
-        square(1, 1)
-        scores(1, 2)
-        scores(1, 3)
-        quantise("m", 1)
         take_q2(1, 0)
-        weights(1, 1)
+        square(1, 0)
         products(0, 0, 1)
         products(0, 1, 1)
+        scores(1, 2)
+        scores(1, 3)
         turn_q2(1, 1)
-        take_relu(1, 2)
-        square(1, 2)
-        finish(0, 0, 1)
-        quantise("aq", 1, 0)
         products(0, 2, 1)
         products(0, 3, 1)
+        finish(0, 0, 1)
         finish(0, 1, 1)
-        take_relu(1, 3)
-        square(1, 3)
-        take_q2(1, 1)
-        weights(1, 2)
-        products(1, 0, 0)
-        products(1, 0, 1)
+        weights(1, 0)
         finish(0, 2, 1)
-        weights(1, 3)
-        products(1, 1, 0)
-        products(1, 1, 1)
+        quantise("aq", 1, 0)
         finish(0, 3, 1)
-        quantise("aq", 1, 1)
+        take_relu(1, 2)
+        take_q2(1, 1)
+        square(1, 1, 0, 1)
+        take_relu(1, 3)
+        square(1, 1, 1, 2)
         for j in range(2):
             for h in range(HALVES):
-                finish(1, j, h)
-                products(1, 2 + j, h)
-        for j in range(2, 4):
-            for h in range(HALVES):
-                finish(1, j, h)
+                products(1, j, h)
+        weights(1, 1, 0, 1)
+        quantise_columns(("aq", 1, 1), 2 * P, 4 * P)
+        finish(1, 0, 0)
+        quantise_columns(("aq", 1, 1), 0, P)
+        finish(1, 0, 1)
+        products(1, 2, 0)
+        products(1, 2, 1)
+        weights(1, 1, 1, 2)
+        finish(1, 1, 0)
+        quantise_columns(("aq", 1, 1), P, 2 * P)
+        finish(1, 1, 1)
+        products(1, 3, 0)
+        products(1, 3, 1)
+        finish(1, 2, 0)
+        finish(1, 2, 1)
+        finish(1, 3, 0)
+        finish(1, 3, 1, 2)

@@ -73,7 +73,7 @@ def tile_flashmixedchunkrelusquaredplusgloballine_kernel(tc, q1, k1, q2, k2, v_b
             for t in range(lo, hi):
                 vb[c, h, t] = tile[:, t - lo, :]
 
-        nc.scalar.dma_start(out=vs[:], in_=v_scale.rearrange("o (c p t) x -> p (o c) (t x)", p=P, t=PACK))
+        nc.sync.dma_start(out=vs[:], in_=v_scale.rearrange("o (c p t) x -> p (o c) (t x)", p=P, t=PACK))
         nc.scalar.activation(out=ident_f32[:], in_=ident_bf[:], func=ACT.Copy)
         load_v(0, 0, 0, 2)
         load_v(0, 0, 2, PACK)
@@ -250,10 +250,10 @@ def tile_flashmixedchunkrelusquaredplusgloballine_kernel(tc, q1, k1, q2, k2, v_b
         quantise("v", 0)
         for j in range(4):
             scores(0, j)
-        widen_scalar(1, 1, (0, 1, 2))
+        widen_scalar(1, 1, (0, 1))
         turn_q2(0, 0)
         widen_vector(0, 1, (2, 3))
-        widen_vector(1, 1, (3,))
+        widen_vector(1, 1, (2, 3))
         take_relu(0, 0)
         take_relu(0, 1)
         turn("k1", 1)

@@ -20,30 +20,40 @@ PACK = 4
 HALF = 512
 CHUNKS = T // C
 HALVES = E // HALF
+PAIRS = PACK // 2
 BANKS = 8
+RESULT_BUFFERS = 8
+RUN = 4
+
+FIRST_VECTOR_PLANES = 3
+LATE_SCALAR_PLANES = 2
+VECTOR_COLUMNS = HALF // 2
 
 
 def tile_flashmixedchunkrelusquaredplusgloballine_kernel(tc, q1, k1, q2, k2, v_bytes, v_scale, gt, u, out):
     nc = tc.nc
 
-    def rows(x, c):
+    def planes(x, c):
         return x[0, c * C:(c + 1) * C, :].rearrange("(p t) w -> p t w", t=PACK)
+
+    def block(i):
+        return slice(i * P, (i + 1) * P)
+
+    def label(key):
+        return "_".join(str(s) for s in key)
 
     with ExitStack() as ctx:
         keep = ctx.enter_context(tc.tile_pool(name="keep", bufs=1))
-        stage = ctx.enter_context(tc.tile_pool(name="stage", bufs=8))
+        results = ctx.enter_context(tc.tile_pool(name="results", bufs=RESULT_BUFFERS))
         psum = ctx.enter_context(tc.psum_pool(name="psum", bufs=1))
         ctx.enter_context(tc.manual_schedule())
+
+        def kept(key, shape, dtype):
+            return keep.tile(shape, dtype, name=label(key), align_bytes=64)
 
         free_banks = list(range(BANKS))
         bank_of = {}
         in_psum = {}
-
-        def label(key):
-            return "_".join(str(s) for s in key)
-
-        def kept(key, shape, dtype):
-            return keep.tile(shape, dtype, name=label(key), align_bytes=64)
 
         def take_bank(key, shape, dtype):
             bank_of[key] = free_banks.pop(0)
@@ -60,23 +70,23 @@ def tile_flashmixedchunkrelusquaredplusgloballine_kernel(tc, q1, k1, q2, k2, v_b
         vs = kept(("vs",), [P, CHUNKS, PACK], F32)
         gt_raw = kept(("gt_raw",), [P, CHUNKS, PACK], BF16)
         gain = kept(("gain",), [P, CHUNKS, PACK], F32)
-        vb = {}
+        v_plane = {}
         raw = {}
 
         def load(name, x, c, width):
             raw[name, c] = kept(("raw", name, c), [P, PACK, width], BF16)
-            nc.sync.dma_start(out=raw[name, c][:], in_=rows(x, c))
+            nc.sync.dma_start(out=raw[name, c][:], in_=planes(x, c))
 
         def load_v(c, h, lo, hi):
             tile = kept(("vbytes", c, h, lo), [P, hi - lo, HALF], U8)
-            nc.sync.dma_start(out=tile[:], in_=rows(v_bytes, c)[:, lo:hi, h * HALF:(h + 1) * HALF])
+            nc.sync.dma_start(out=tile[:], in_=planes(v_bytes, c)[:, lo:hi, h * HALF:(h + 1) * HALF])
             for t in range(lo, hi):
-                vb[c, h, t] = tile[:, t - lo, :]
+                v_plane[c, h, t] = tile[:, t - lo, :]
 
         nc.sync.dma_start(out=vs[:], in_=v_scale.rearrange("o (c p t) x -> p (o c) (t x)", p=P, t=PACK))
         nc.scalar.activation(out=ident_f32[:], in_=ident_bf[:], func=ACT.Copy)
-        load_v(0, 0, 0, 2)
-        load_v(0, 0, 2, PACK)
+        load_v(0, 0, 0, PACK // 2)
+        load_v(0, 0, PACK // 2, PACK)
         load_v(1, 0, 0, PACK)
         load("k2", k2, 0, M)
         load("k2", k2, 1, M)
@@ -102,7 +112,7 @@ def tile_flashmixedchunkrelusquaredplusgloballine_kernel(tc, q1, k1, q2, k2, v_b
         for c in range(CHUNKS):
             for h in range(HALVES):
                 wide[c, h] = kept(("wide", c, h), [P, PACK, HALF], BF16)
-            for pair in range(2):
+            for pair in range(PAIRS):
                 grouped["aq", c, pair] = kept(("grouped_aq", c, pair), [P, 4 * P * PACK], BF16)
                 relu[c, pair] = kept(("relu", c, pair), [P, 2, P * PACK], F32)
                 squared[c, pair] = kept(("squared", c, pair), [P, 2, P * PACK], F32)
@@ -110,7 +120,6 @@ def tile_flashmixedchunkrelusquaredplusgloballine_kernel(tc, q1, k1, q2, k2, v_b
             grouped["m", h] = kept(("grouped_m", h), [P, HALF * PACK], BF16)
             grouped["v", h] = kept(("grouped_v", h), [P, CHUNKS * HALF * PACK], BF16)
         grouped["k2",] = kept(("grouped_k2",), [P, CHUNKS * M * PACK], BF16)
-
         for key in grouped:
             codes[key] = kept(("codes",) + key, [P, grouped[key].shape[1] // PACK], U32)
             scales[key] = kept(("scales",) + key, [P, grouped[key].shape[1] // PACK], U8)
@@ -122,19 +131,20 @@ def tile_flashmixedchunkrelusquaredplusgloballine_kernel(tc, q1, k1, q2, k2, v_b
         def quantise(*key):
             quantise_columns(key, 0, codes[key].shape[1])
 
-        def widen_scalar(c, h, planes):
-            for t in planes:
-                nc.scalar.activation(out=wide[c, h][:, t, :], in_=vb[c, h, t].bitcast(FP8),
+        def widen_scalar(c, h, lo, hi):
+            for t in range(lo, hi):
+                nc.scalar.activation(out=wide[c, h][:, t, :], in_=v_plane[c, h, t].bitcast(FP8),
                                      func=ACT.Copy, scale=vs[:, c, t:t + 1])
 
-        def widen_vector(c, h, planes):
-            for t in planes:
-                nc.vector.tensor_scalar(out=wide[c, h][:, t, :], in0=vb[c, h, t].bitcast(FP8),
+        def widen_vector(c, h, lo, hi):
+            for t in range(lo, hi):
+                nc.vector.tensor_scalar(out=wide[c, h][:, t, :], in0=v_plane[c, h, t].bitcast(FP8),
                                         scalar1=vs[:, c, t:t + 1], scalar2=None, op0=ALU.mult)
 
         def interleave_v(copy, c, h, lo, hi):
-            copy(out=grouped["v", h][:, (c * HALF + lo) * PACK:(c * HALF + hi) * PACK].rearrange("p (e i t) -> p e t i", i=4, t=PACK),
-                 in_=wide[c, h][:, :, lo:hi].rearrange("p t (e i) -> p e t i", i=4))
+            dst = grouped["v", h][:, (c * HALF + lo) * PACK:(c * HALF + hi) * PACK]
+            copy(out=dst.rearrange("p (e i t) -> p e t i", i=RUN, t=PACK),
+                 in_=wide[c, h][:, :, lo:hi].rearrange("p t (e i) -> p e t i", i=RUN))
 
         def interleave_k2(c):
             nc.vector.tensor_copy(
@@ -143,11 +153,6 @@ def tile_flashmixedchunkrelusquaredplusgloballine_kernel(tc, q1, k1, q2, k2, v_b
 
         def make_gain():
             nc.vector.tensor_scalar(out=gain[:], in0=gt_raw[:], scalar1=1.0 / D, scalar2=None, op0=ALU.mult)
-
-        def warm_up(i):
-            b = take_bank(("warm", i), [P, HALF], F32)
-            nc.tensor.matmul(out=b[:], lhsT=ident_bf[:], rhs=raw["k2", 0][:, 0, :], start=True, stop=True)
-            free_bank(("warm", i))
 
         def turn(name, c):
             b = take_bank(("turn", name, c), [P, PACK, P], BF16)
@@ -199,9 +204,6 @@ def tile_flashmixedchunkrelusquaredplusgloballine_kernel(tc, q1, k1, q2, k2, v_b
                 out=acc, lhsT=codes[lhs][:, lhs_cols].bitcast(FP8X4), lhsT_scale=scales[lhs][:, lhs_cols],
                 rhs=codes[rhs][:, rhs_cols].bitcast(FP8X4), rhs_scale=scales[rhs][:, rhs_cols], start=start, stop=stop)
 
-        def block(i):
-            return slice(i * P, (i + 1) * P)
-
         def memory(h, e):
             b = take_bank(("m", h, e), [P, PACK, P], F32)
             for s in range(PACK):
@@ -222,48 +224,47 @@ def tile_flashmixedchunkrelusquaredplusgloballine_kernel(tc, q1, k1, q2, k2, v_b
         def finish(c, j, h, parts=1):
             width = HALF // parts
             for part in range(parts):
-                res = stage.tile([P, width], F32, name=label(("res", c, j, h, part)), tag="res")
+                res = results.tile([P, width], F32, name=label(("res", c, j, h, part)), tag="res")
                 span = slice(h * HALF + part * width, h * HALF + (part + 1) * width)
                 nc.vector.tensor_tensor(out=res[:], in0=in_psum["o", c, j, h][:, part * width:(part + 1) * width],
                                         in1=raw["u", c][:, j, span], op=ALU.mult)
-                nc.sync.dma_start(out=rows(out, c)[:, j, span], in_=res[:])
+                nc.sync.dma_start(out=planes(out, c)[:, j, span], in_=res[:])
             free_bank(("o", c, j, h))
 
-        widen_vector(0, 0, (0, 1, 2))
-        widen_scalar(0, 0, (3,))
-        widen_scalar(1, 0, (0, 1, 2, 3))
+
+        widen_vector(0, 0, 0, FIRST_VECTOR_PLANES)
+        widen_scalar(0, 0, FIRST_VECTOR_PLANES, PACK)
+        widen_scalar(1, 0, 0, PACK)
         interleave_v(nc.vector.tensor_copy, 0, 0, 0, HALF)
         interleave_k2(0)
-        warm_up(0)
-        warm_up(1)
-        interleave_v(nc.scalar.copy, 1, 0, HALF // 2, HALF)
+        interleave_v(nc.scalar.copy, 1, 0, VECTOR_COLUMNS, HALF)
         interleave_k2(1)
         turn("k1", 0)
         turn("q1", 0)
-        warm_up(2)
         take_turned("k1", 0)
-        widen_scalar(0, 1, (0,))
+        widen_scalar(0, 1, 0, 1)
         take_turned("q1", 0)
-        widen_scalar(0, 1, (1,))
-        interleave_v(nc.vector.tensor_copy, 1, 0, 0, HALF // 2)
+        widen_scalar(0, 1, 1, LATE_SCALAR_PLANES)
+        interleave_v(nc.vector.tensor_copy, 1, 0, 0, VECTOR_COLUMNS)
         quantise("k2")
         quantise("v", 0)
-        for j in range(4):
+
+        for j in range(PACK):
             scores(0, j)
-        widen_scalar(1, 1, (0, 1))
+        widen_scalar(1, 1, 0, LATE_SCALAR_PLANES)
         turn_q2(0, 0)
-        widen_vector(0, 1, (2, 3))
-        widen_vector(1, 1, (2, 3))
+        for c in range(CHUNKS):
+            widen_vector(c, 1, LATE_SCALAR_PLANES, PACK)
         take_relu(0, 0)
         take_relu(0, 1)
         turn("k1", 1)
         turn("q1", 1)
         memory(0, 0)
         memory(0, 1)
-        take_q2(0, 0)
         square(0, 0)
-        interleave_v(nc.vector.tensor_copy, 0, 1, 0, HALF)
-        interleave_v(nc.vector.tensor_copy, 1, 1, 0, HALF)
+        take_q2(0, 0)
+        for c in range(CHUNKS):
+            interleave_v(nc.vector.tensor_copy, c, 1, 0, HALF)
         take_relu(0, 2)
         take_relu(0, 3)
         memory(0, 2)
@@ -274,21 +275,23 @@ def tile_flashmixedchunkrelusquaredplusgloballine_kernel(tc, q1, k1, q2, k2, v_b
         square(0, 1)
         make_gain()
         quantise("v", 1)
-        weights(0, 0)
-        weights(0, 1)
-        for e in range(4):
+
+        for pair in range(PAIRS):
+            weights(0, pair)
+        for e in range(PACK):
             take_memory(0, e)
         scores(1, 0)
         scores(1, 1)
         take_q2(0, 1)
-        for e in range(4):
+        for e in range(PACK):
             memory(1, e)
         quantise("aq", 0, 0)
         quantise("m", 0)
         quantise("aq", 0, 1)
-        for e in range(4):
+
+        for e in range(PACK):
             take_memory(1, e)
-        for j in range(4):
+        for j in range(PACK):
             products(0, j, 0)
         turn_q2(1, 0)
         take_relu(1, 0)
@@ -298,6 +301,7 @@ def tile_flashmixedchunkrelusquaredplusgloballine_kernel(tc, q1, k1, q2, k2, v_b
         quantise("m", 1)
         finish(0, 2, 0)
         finish(0, 3, 0)
+
         take_q2(1, 0)
         square(1, 0)
         products(0, 0, 1)
@@ -313,6 +317,7 @@ def tile_flashmixedchunkrelusquaredplusgloballine_kernel(tc, q1, k1, q2, k2, v_b
         finish(0, 2, 1)
         quantise("aq", 1, 0)
         finish(0, 3, 1)
+
         take_relu(1, 2)
         take_q2(1, 1)
         square(1, 1, 0, 1)
@@ -321,20 +326,17 @@ def tile_flashmixedchunkrelusquaredplusgloballine_kernel(tc, q1, k1, q2, k2, v_b
         for j in range(2):
             for h in range(HALVES):
                 products(1, j, h)
-        weights(1, 1, 0, 1)
-        quantise_columns(("aq", 1, 1), 2 * P, 4 * P)
-        finish(1, 0, 0)
-        quantise_columns(("aq", 1, 1), 0, P)
-        finish(1, 0, 1)
-        products(1, 2, 0)
-        products(1, 2, 1)
-        weights(1, 1, 1, 2)
-        finish(1, 1, 0)
-        quantise_columns(("aq", 1, 1), P, 2 * P)
-        finish(1, 1, 1)
-        products(1, 3, 0)
-        products(1, 3, 1)
+        for j in range(2):
+            weights(1, 1, j, j + 1)
+            if j == 0:
+                quantise_columns(("aq", 1, 1), 2 * P, 4 * P)
+            finish(1, j, 0)
+            quantise_columns(("aq", 1, 1), j * P, (j + 1) * P)
+            finish(1, j, 1)
+            for h in range(HALVES):
+                products(1, 2 + j, h)
+
         finish(1, 2, 0)
         finish(1, 2, 1)
         finish(1, 3, 0)
-        finish(1, 3, 1, 2)
+        finish(1, 3, 1, parts=2)

from contextlib import ExitStack

import concourse.mybir as mybir
from concourse.masks import make_identity

T, C, D, M, E = 1024, 512, 128, 512, 1024
FLOPS = 2 * T * C * D + 2 * T * C * E + 2 * T * M * E + 2 * T * M * E

F32 = mybir.dt.float32
BF16 = mybir.dt.bfloat16
U32 = mybir.dt.uint32
U8 = mybir.dt.uint8
FP8 = mybir.dt.float8_e4m3fn
FP8X4 = mybir.dt.float8_e4m3fn_x4
ALU = mybir.AluOpType
ACT = mybir.ActivationFunctionType

P = 128
PACK = 4
HALF = 512
CHUNKS = T // C
HALVES = E // HALF
PAIRS = PACK // 2
BANKS = 8
RESULT_BUFFERS = 8
RUN = 4

FIRST_VECTOR_PLANES = 3
LATE_SCALAR_PLANES = 2
VECTOR_COLUMNS = HALF // 2


def tile_flashmixedchunkrelusquaredplusgloballine_kernel(tc, q1, k1, q2, k2, v_bytes, v_scale, gt, u, out):
    nc = tc.nc

    def planes(x, c):
        return x[0, c * C:(c + 1) * C, :].rearrange("(p t) w -> p t w", t=PACK)

    def block(i):
        return slice(i * P, (i + 1) * P)

    def label(key):
        return "_".join(str(s) for s in key)

    with ExitStack() as ctx:
        keep = ctx.enter_context(tc.tile_pool(name="keep", bufs=1))
        results = ctx.enter_context(tc.tile_pool(name="results", bufs=RESULT_BUFFERS))
        psum = ctx.enter_context(tc.psum_pool(name="psum", bufs=1))
        ctx.enter_context(tc.manual_schedule())

        def kept(key, shape, dtype):
            return keep.tile(shape, dtype, name=label(key), align_bytes=64)

        free_banks = list(range(BANKS))
        bank_of = {}
        in_psum = {}

        def take_bank(key, shape, dtype):
            bank_of[key] = free_banks.pop(0)
            in_psum[key] = psum.tile(shape, dtype, name=label(key), tag="bank%d" % bank_of[key])
            return in_psum[key]

        def free_bank(key):
            free_banks.append(bank_of[key])

        ident_bf = kept(("ident_bf",), [P, P], BF16)
        ident_f32 = kept(("ident_f32",), [P, P], F32)
        make_identity(nc, ident_bf[:])

        vs = kept(("vs",), [P, CHUNKS, PACK], F32)
        gt_raw = kept(("gt_raw",), [P, CHUNKS, PACK], BF16)
        gain = kept(("gain",), [P, CHUNKS, PACK], F32)
        v_plane = {}
        raw = {}

        def load(name, x, c, width):
            raw[name, c] = kept(("raw", name, c), [P, PACK, width], BF16)
            nc.sync.dma_start(out=raw[name, c][:], in_=planes(x, c))

        def load_v(c, h, lo, hi):
            tile = kept(("vbytes", c, h, lo), [P, hi - lo, HALF], U8)
            nc.sync.dma_start(out=tile[:], in_=planes(v_bytes, c)[:, lo:hi, h * HALF:(h + 1) * HALF])
            for t in range(lo, hi):
                v_plane[c, h, t] = tile[:, t - lo, :]

        nc.sync.dma_start(out=vs[:], in_=v_scale.rearrange("o (c p t) x -> p (o c) (t x)", p=P, t=PACK))
        nc.scalar.activation(out=ident_f32[:], in_=ident_bf[:], func=ACT.Copy)
        load_v(0, 0, 0, PACK // 2)
        load_v(0, 0, PACK // 2, PACK)
        load_v(1, 0, 0, PACK)
        load("k2", k2, 0, M)
        load("k2", k2, 1, M)
        load("k1", k1, 0, D)
        load("q1", q1, 0, D)
        load_v(0, 1, 0, PACK)
        nc.sync.dma_start(out=gt_raw[:], in_=gt.rearrange("(c p t) -> p c t", p=P, t=PACK))
        load_v(1, 1, 0, PACK)
        load("q2", q2, 0, M)
        load("k1", k1, 1, D)
        load("q1", q1, 1, D)
        load("u", u, 0, E)
        load("q2", q2, 1, M)
        load("u", u, 1, E)

        wide = {}
        grouped = {}
        codes = {}
        scales = {}
        turned = {}
        relu = {}
        squared = {}
        for c in range(CHUNKS):
            for h in range(HALVES):
                wide[c, h] = kept(("wide", c, h), [P, PACK, HALF], BF16)
            for pair in range(PAIRS):
                grouped["aq", c, pair] = kept(("grouped_aq", c, pair), [P, 4 * P * PACK], BF16)
                relu[c, pair] = kept(("relu", c, pair), [P, 2, P * PACK], F32)
                squared[c, pair] = kept(("squared", c, pair), [P, 2, P * PACK], F32)
        for h in range(HALVES):
            grouped["m", h] = kept(("grouped_m", h), [P, HALF * PACK], BF16)
            grouped["v", h] = kept(("grouped_v", h), [P, CHUNKS * HALF * PACK], BF16)
        grouped["k2",] = kept(("grouped_k2",), [P, CHUNKS * M * PACK], BF16)
        for key in grouped:
            codes[key] = kept(("codes",) + key, [P, grouped[key].shape[1] // PACK], U32)
            scales[key] = kept(("scales",) + key, [P, grouped[key].shape[1] // PACK], U8)

        def quantise_columns(key, lo, hi):
            nc.vector.quantize_mx(out=codes[key][:, lo:hi].bitcast(FP8X4), scales=scales[key][:, lo:hi],
                                  in_=grouped[key][:, lo * PACK:hi * PACK])

        def quantise(*key):
            quantise_columns(key, 0, codes[key].shape[1])

        def widen_scalar(c, h, lo, hi):
            for t in range(lo, hi):
                nc.scalar.activation(out=wide[c, h][:, t, :], in_=v_plane[c, h, t].bitcast(FP8),
                                     func=ACT.Copy, scale=vs[:, c, t:t + 1])

        def widen_vector(c, h, lo, hi):
            for t in range(lo, hi):
                nc.vector.tensor_scalar(out=wide[c, h][:, t, :], in0=v_plane[c, h, t].bitcast(FP8),
                                        scalar1=vs[:, c, t:t + 1], scalar2=None, op0=ALU.mult)

        def interleave_v(copy, c, h, lo, hi):
            dst = grouped["v", h][:, (c * HALF + lo) * PACK:(c * HALF + hi) * PACK]
            copy(out=dst.rearrange("p (e i t) -> p e t i", i=RUN, t=PACK),
                 in_=wide[c, h][:, :, lo:hi].rearrange("p t (e i) -> p e t i", i=RUN))

        def interleave_k2(c):
            nc.vector.tensor_copy(
                out=grouped["k2",][:, c * M * PACK:(c + 1) * M * PACK].rearrange("p (s b i t) -> p b s i t", s=PACK, i=2, t=PACK),
                in_=raw["k2", c][:].rearrange("p t (b i s) -> p b s i t", i=2, s=PACK))

        def make_gain():
            nc.vector.tensor_scalar(out=gain[:], in0=gt_raw[:], scalar1=1.0 / D, scalar2=None, op0=ALU.mult)

        def turn(name, c):
            b = take_bank(("turn", name, c), [P, PACK, P], BF16)
            for t in range(PACK):
                nc.tensor.transpose(b[:, t, :], raw[name, c][:, t, :], ident_bf[:])

        def take_turned(name, c):
            turned[name, c] = kept(("turned", name, c), [P, PACK, P], BF16)
            nc.scalar.copy(out=turned[name, c][:], in_=in_psum["turn", name, c][:])
            free_bank(("turn", name, c))

        def scores(c, j):
            z = take_bank(("z", c, j), [P, PACK, P], F32)
            for t in range(PACK):
                nc.tensor.matmul(out=z[:, t, :], lhsT=turned["k1", c][:, t, :], rhs=turned["q1", c][:, j, :],
                                 start=True, stop=True)

        def take_relu(c, j):
            nc.scalar.activation(out=relu[c, j // 2][:, j % 2, :].rearrange("p (n t) -> p n t", t=PACK),
                                 in_=in_psum["z", c, j][:].rearrange("p t n -> p n t"), func=ACT.Relu)
            free_bank(("z", c, j))

        def square(c, pair, lo=0, hi=2):
            nc.scalar.activation(out=squared[c, pair][:, lo:hi, :], in_=relu[c, pair][:, lo:hi, :], func=ACT.Square)

        def weights(c, pair, lo=0, hi=2):
            dst = grouped["aq", c, pair][:].rearrange("p (x j n t) -> p x j n t", j=2, x=2, t=PACK)
            nc.vector.tensor_tensor(
                out=dst[:, 0, lo:hi, :, :],
                in0=squared[c, pair][:, lo:hi, :].rearrange("p j (n t) -> p j n t", t=PACK),
                in1=gain[:, c:c + 1, :].unsqueeze(1).to_broadcast([P, hi - lo, P, PACK]), op=ALU.mult)

        def turn_q2(c, pair):
            b = take_bank(("turn_q2", c, pair), [P, 2, 2, P], F32)
            words = raw["q2", c][:].rearrange("p t m -> p (t m)").bitcast(F32)
            for jj in range(2):
                base = (2 * pair + jj) * (M // 2)
                for s in range(2):
                    nc.tensor.transpose(b[:, jj, s, :], words[:, base + s:base + M // 2:2], ident_f32[:])

        def take_q2(c, pair):
            nc.scalar.copy(
                out=grouped["aq", c, pair][:, 2 * P * PACK:].bitcast(F32).rearrange("p (j n s) -> p j n s", j=2, s=2),
                in_=in_psum["turn_q2", c, pair][:].rearrange("p j s n -> p j n s"))
            free_bank(("turn_q2", c, pair))

        def mx(acc, lhs, lhs_cols, rhs, rhs_cols, start, stop):
            nc.tensor.matmul_mx(
                out=acc, lhsT=codes[lhs][:, lhs_cols].bitcast(FP8X4), lhsT_scale=scales[lhs][:, lhs_cols],
                rhs=codes[rhs][:, rhs_cols].bitcast(FP8X4), rhs_scale=scales[rhs][:, rhs_cols], start=start, stop=stop)

        def memory(h, e):
            b = take_bank(("m", h, e), [P, PACK, P], F32)
            for s in range(PACK):
                for c in range(CHUNKS):
                    mx(b[:, s, :], ("k2",), block(PACK * c + s), ("v", h), block(PACK * c + e), c == 0, c == CHUNKS - 1)

        def take_memory(h, e):
            dst = grouped["m", h][:, e * P * PACK:(e + 1) * P * PACK]
            nc.scalar.copy(out=dst.rearrange("p (x s) -> p x s", s=PACK),
                           in_=in_psum["m", h, e][:].rearrange("p s x -> p x s"))
            free_bank(("m", h, e))

        def products(c, j, h):
            b = take_bank(("o", c, j, h), [P, HALF], F32)
            mx(b[:], ("aq", c, j // 2), block(j % 2), ("v", h), slice(c * HALF, (c + 1) * HALF), True, False)
            mx(b[:], ("aq", c, j // 2), block(2 + j % 2), ("m", h), slice(0, HALF), False, True)

        def finish(c, j, h, parts=1):
            width = HALF // parts
            for part in range(parts):
                res = results.tile([P, width], F32, name=label(("res", c, j, h, part)), tag="res")
                span = slice(h * HALF + part * width, h * HALF + (part + 1) * width)
                nc.vector.tensor_tensor(out=res[:], in0=in_psum["o", c, j, h][:, part * width:(part + 1) * width],
                                        in1=raw["u", c][:, j, span], op=ALU.mult)
                nc.sync.dma_start(out=planes(out, c)[:, j, span], in_=res[:])
            free_bank(("o", c, j, h))


        widen_vector(0, 0, 0, FIRST_VECTOR_PLANES)
        widen_scalar(0, 0, FIRST_VECTOR_PLANES, PACK)
        widen_scalar(1, 0, 0, PACK)
        interleave_v(nc.vector.tensor_copy, 0, 0, 0, HALF)
        interleave_k2(0)
        interleave_v(nc.scalar.copy, 1, 0, VECTOR_COLUMNS, HALF)
        interleave_k2(1)
        turn("k1", 0)
        turn("q1", 0)
        take_turned("k1", 0)
        widen_scalar(0, 1, 0, 1)
        take_turned("q1", 0)
        widen_scalar(0, 1, 1, LATE_SCALAR_PLANES)
        interleave_v(nc.vector.tensor_copy, 1, 0, 0, VECTOR_COLUMNS)
        quantise("k2")
        quantise("v", 0)

        for j in range(PACK):
            scores(0, j)
        widen_scalar(1, 1, 0, LATE_SCALAR_PLANES)
        turn_q2(0, 0)
        for c in range(CHUNKS):
            widen_vector(c, 1, LATE_SCALAR_PLANES, PACK)
        take_relu(0, 0)
        take_relu(0, 1)
        turn("k1", 1)
        turn("q1", 1)
        memory(0, 0)
        memory(0, 1)
        square(0, 0)
        take_q2(0, 0)
        for c in range(CHUNKS):
            interleave_v(nc.vector.tensor_copy, c, 1, 0, HALF)
        take_relu(0, 2)
        take_relu(0, 3)
        memory(0, 2)
        memory(0, 3)
        turn_q2(0, 1)
        take_turned("k1", 1)
        take_turned("q1", 1)
        square(0, 1)
        make_gain()
        quantise("v", 1)

        for pair in range(PAIRS):
            weights(0, pair)
        for e in range(PACK):
            take_memory(0, e)
        scores(1, 0)
        scores(1, 1)
        take_q2(0, 1)
        for e in range(PACK):
            memory(1, e)
        quantise("aq", 0, 0)
        quantise("m", 0)
        quantise("aq", 0, 1)

        for e in range(PACK):
            take_memory(1, e)
        for j in range(PACK):
            products(0, j, 0)
        turn_q2(1, 0)
        take_relu(1, 0)
        take_relu(1, 1)
        finish(0, 0, 0)
        finish(0, 1, 0)
        quantise("m", 1)
        finish(0, 2, 0)
        finish(0, 3, 0)

        take_q2(1, 0)
        square(1, 0)
        products(0, 0, 1)
        products(0, 1, 1)
        scores(1, 2)
        scores(1, 3)
        turn_q2(1, 1)
        products(0, 2, 1)
        products(0, 3, 1)
        finish(0, 0, 1)
        finish(0, 1, 1)
        weights(1, 0)
        finish(0, 2, 1)
        quantise("aq", 1, 0)
        finish(0, 3, 1)

        take_relu(1, 2)
        take_q2(1, 1)
        square(1, 1, 0, 1)
        take_relu(1, 3)
        square(1, 1, 1, 2)
        for j in range(2):
            for h in range(HALVES):
                products(1, j, h)
        for j in range(2):
            weights(1, 1, j, j + 1)
            if j == 0:
                quantise_columns(("aq", 1, 1), 2 * P, 4 * P)
            finish(1, j, 0)
            quantise_columns(("aq", 1, 1), j * P, (j + 1) * P)
            finish(1, j, 1)
            for h in range(HALVES):
                products(1, 2 + j, h)

        finish(1, 2, 0)
        finish(1, 2, 1)
        finish(1, 3, 0)
        finish(1, 3, 1, parts=2)
